import numpy as np
import ml_dtypes


def mxq(x, axis, fmt="e4m3"):
    dtype, down = {"e4m3": (ml_dtypes.float8_e4m3fn, 7), "e5m2": (ml_dtypes.float8_e5m2, 14)}[fmt]
    v = np.moveaxis(np.asarray(x, np.float32).astype(ml_dtypes.bfloat16).astype(np.float64), axis, -1)
    blocks = v.reshape(v.shape[:-1] + (-1, 32))
    amax = np.abs(blocks).max(-1, keepdims=True)
    byte = np.maximum(np.where(amax > 0, np.frexp(amax)[1] - 1 + 127, 0) - down, 1)
    scale = np.exp2(byte - 127.0)
    codes = (blocks / scale).astype(np.float32).astype(dtype).astype(np.float64)
    return np.moveaxis((codes * scale).reshape(v.shape), -1, axis)


WIDE = False


def mx_kscale(k):
    if not WIDE:
        return np.ones(k)
    levels = np.array([10, -10, 5, -5, 0])
    if k % 512:
        return np.exp2(np.random.permutation(np.resize(levels, k // 32))).repeat(32)
    a = np.empty((k // 512, 16))
    for p in range(k // 512):
        a[p, :8] = np.random.permutation(np.resize(levels, 8))
        for g in range(8):
            far = levels[np.abs(levels - a[p, g]) >= 10]
            a[p, g + 8] = far[np.random.randint(len(far))]
    return np.exp2(a.ravel()).repeat(32)


def f64(x):
    return np.asarray(x).astype(np.float64)


def striped(idx):
    return np.tile(np.asarray(idx).reshape(-1, 16).T, (8, 1)).astype(np.uint16)


def unstriped(offs):
    return offs[:16].T.reshape(-1).astype(np.int64)


E2M1 = np.array([0.0, 0.5, 1.0, 1.5, 2.0, 3.0, 4.0, 6.0, -0.0, -0.5, -1.0, -1.5, -2.0, -3.0, -4.0, -6.0])


def pack_weight(w, fmt):
    k, n = w.shape
    w = f64(np.asarray(w, np.float32).astype(ml_dtypes.bfloat16)).reshape(k // 32, 32, n)
    amax = np.abs(w).max(1)
    if fmt == "e4m3":
        byte = np.frexp(amax)[1] - 1 + 127 - 7
    else:
        mant, ex = np.frexp(amax / 6.0)
        byte = np.where(mant > 0.5, ex, ex - 1) + 127
    byte = np.clip(np.where(amax > 0, byte, 1), 1, 254)
    scaled = (w * np.exp2(127.0 - byte)[:, None, :]).reshape(k, n).astype(np.float32)
    by_word = np.ascontiguousarray(scaled.reshape(k // 512, 128, 4, n).transpose(0, 1, 3, 2))
    if fmt == "e4m3":
        words = by_word.astype(ml_dtypes.float8_e4m3fn).view(np.uint8)
    else:
        c = by_word.astype(ml_dtypes.float4_e2m1fn).view(np.uint8) & 0xF
        words = (c[..., 0::2] | (c[..., 1::2] << 4)).reshape(k // 512, 128, 2 * n)
    return np.ascontiguousarray(words), np.ascontiguousarray(byte.astype(np.uint8).reshape(k // 512, 16, n))


def unpack_weight(words, scales, fmt):
    g, _, n = scales.shape
    words = np.ascontiguousarray(words).reshape(g, 128, n, -1)
    if fmt == "e4m3":
        vals = words.view(ml_dtypes.float8_e4m3fn).astype(np.float64)
    else:
        nib = np.empty((g, 128, n, 4), np.uint8)
        nib[..., 0::2] = words & 0xF
        nib[..., 1::2] = words >> 4
        vals = E2M1[nib]
    vals = vals * np.repeat(np.exp2(scales.astype(np.float64) - 127.0), 8, axis=1)[..., None]
    return vals.transpose(0, 1, 3, 2).reshape(g * 512, n)


B, N, T, D, NQ = 1, 512, 2048, 1024, 128


def setup_inputs():
    n = np.random.standard_normal
    idx = np.random.permutation(T)[:B * N]
    s = mx_kscale(D)[:, None]
    kp = pack_weight(n((D, T)) / s, "e2m1")
    return {
        "qT": (n((B, D, NQ)) * s * (0.50 / np.sqrt(D))).astype(np.float32),
        "k_words": np.ascontiguousarray(kp[0].reshape(1, 2, 128, T, 2).transpose(0, 2, 3, 1, 4)).reshape(1, 128, T, 4),
        "k_scales": kp[1],
        "kn": np.tile(np.random.uniform(1.0, 4.0, 2048), (128, 1)).astype(np.float32),
        "qn": (np.random.uniform(1.0, 4.0, (B, NQ, 1))).astype(np.float32),
        "offs": striped(idx),
    }


def reference(qT, k_words, k_scales, kn, qn, offs):
    idx = unstriped(offs)
    pick = lambda x, which: x[:, which].reshape(x.shape[0], B, -1).transpose(1, 0, 2)
    k = unpack_weight(k_words.reshape(1, 128, T, 2, 2).transpose(0, 3, 1, 2, 4).reshape(2, 128, 2 * T), k_scales, "e2m1")
    kg = pick(k, idx)
    qq = mxq(f64(qT), 1, "e4m3")
    a = qq.transpose(0, 2, 1) @ kg
    t = 1.0 / (1.0 + np.maximum(f64(qn) + pick(f64(kn), idx)[:, :1, :] - 2.0 * a, 0.0))
    y = t / np.sum(t, axis=-1, keepdims=True)
    return y

@@ -1,0 +1,149 @@
+from contextlib import ExitStack
+
+import concourse.mybir as mybir
+from concourse.masks import make_identity
+
+FLOPS = 2 * 128 * 512 * 1024
+
+F32 = mybir.dt.float32
+BF16 = mybir.dt.bfloat16
+I32 = mybir.dt.int32
+U32 = mybir.dt.uint32
+U16 = mybir.dt.uint16
+U8 = mybir.dt.uint8
+FP8X4 = mybir.dt.float8_e4m3fn_x4
+FP4X4 = mybir.dt.float4_e2m1fn_x4
+ALU = mybir.AluOpType
+ACT = mybir.ActivationFunctionType
+
+P = 128
+T = 2048
+N = 512
+HALF = 256
+TILE = 128
+PASSES = 2
+KN_ROW = 8
+SHIFT = 16
+MOVED_ROWS = 112
+
+
+def tile_attend_student_topk_kernel(tc, qT, k_words, k_scales, kn, qn, offs, out):
+    nc = tc.nc
+    with ExitStack() as ctx:
+        sb = ctx.enter_context(tc.tile_pool(name="sb", bufs=1))
+        reused = ctx.enter_context(tc.tile_pool(name="reused", bufs=1))
+        ps = ctx.enter_context(tc.psum_pool(name="ps", bufs=1))
+
+        offsets = sb.tile([P, N // 16], U16, name="offsets")
+        nc.sync.dma_start(offsets[:], offs)
+        qn_col = sb.tile([P, 1], F32, name="qn_col")
+        nc.sync.dma_start(qn_col[:], qn[0])
+
+        q_raw = sb.tile([P, PASSES, 4, P], F32, name="q_raw")
+        nc.scalar.dma_start(q_raw[:], qT[0].rearrange("(o p j) w -> p o j w", o=PASSES, j=4))
+        scales = sb.tile([P, T], U8, name="scales")
+        nc.vector.memset(scales[:].bitcast(I32), 0)
+        by_row = k_scales.rearrange("o (q r) t -> r q o t", r=4)
+        for r in range(4):
+            nc.sync.dma_start(scales[r:P:SHIFT, :].bitcast(I32), by_row[r].bitcast(I32))
+        words = sb.tile([P, T], I32, name="words")
+        nc.sync.dma_start(words[:], k_words[0].rearrange("p t b -> p (t b)").bitcast(I32))
+
+        kn_all = reused.tile([P, T], F32, name="kn_all", offset=0)
+        nc.vector.memset(kn_all[:], 0.0)
+        nc.scalar.dma_start(kn_all[KN_ROW : KN_ROW + 1, :], kn[0:1, :])
+
+        plane1 = sb.tile([P, N], U8, name="plane1", align_bytes=64)
+        nc.vector.memset(plane1[:].bitcast(I32), 0)
+
+        seed = sb.tile([P, 1], F32, name="seed", tag="ident")
+        nc.vector.memset(seed[:], 1.0)
+        warm = sb.tile([P, 1], F32, name="warm")
+        nc.scalar.activation(warm[:], seed[:], ACT.Abs_reciprocal_sqrt, bias=1.0)
+        ident = sb.tile([P, P], F32, name="ident", tag="ident")
+        make_identity(nc, ident[:])
+
+        plane0 = sb.tile([P, N], U8, name="plane0", align_bytes=64)
+        nc.vector.tensor_copy(plane0[:], scales[:].indirect(offsets[:]))
+        nc.sync.dma_start(
+            plane1[0:MOVED_ROWS, :].bitcast(I32),
+            plane0[SHIFT : SHIFT + MOVED_ROWS, :].bitcast(I32),
+        )
+        planes = (plane0, plane1)
+
+        kn_listed = sb.tile([P, N], F32, name="kn_listed")
+        nc.vector.tensor_copy(kn_listed[:], kn_all[:].indirect(offsets[:]))
+
+        q_codes = reused.tile([P, PASSES, P], U32, name="q_codes", align_bytes=64, offset=0)
+        q_planes = reused.tile([P, PASSES, P], U8, name="q_planes", align_bytes=64, offset=1024)
+        for o in range(PASSES):
+            q_bf = sb.tile([P, P, 4], BF16, name="q_bf%d" % o, align_bytes=64)
+            nc.scalar.copy(
+                q_bf[:].rearrange("p (c i) t -> p c t i", i=4),
+                q_raw[:, o].rearrange("p t (c i) -> p c t i", i=4),
+            )
+            nc.vector.quantize_mx(
+                out=q_codes[:, o, :].bitcast(FP8X4),
+                scales=q_planes[:, o, :],
+                in_=q_bf[:].rearrange("p w t -> p (w t)"),
+            )
+
+        kn_turned = ps.tile([P, N // TILE, TILE], F32, name="kn_turned", tag="bank0")
+        for j in range(N // TILE):
+            nc.tensor.transpose(kn_turned[:, j, :], kn_listed[:, j * TILE : (j + 1) * TILE], ident[:])
+        kn_cols = sb.tile([P, N // TILE], F32, name="kn_cols")
+        nc.scalar.copy(kn_cols[:], kn_turned[:, :, KN_ROW])
+        kn_spread = ps.tile([P, N // TILE, TILE], F32, name="kn_spread")
+        for j in range(N // TILE):
+            nc.tensor.transpose(kn_spread[:, j, :], kn_cols[:, j : j + 1].to_broadcast([P, P]), ident[:])
+        kn_rows = sb.tile([P, N], F32, name="kn_rows")
+        nc.scalar.copy(kn_rows[:], kn_spread[:].rearrange("p j n -> p (j n)"))
+
+        dots = []
+        for h in range(2):
+            picked = reused.tile([P, HALF], U32, name="picked%d" % h, offset=2048 + 1024 * h)
+            cols = slice(h * HALF // 16, (h + 1) * HALF // 16)
+            nc.vector.tensor_copy(picked[:], words[:].bitcast(U32).indirect(offsets[:, cols]))
+            k_codes = sb.tile([P, PASSES, HALF], U16, name="k_codes%d" % h, align_bytes=64)
+            nc.vector.tensor_copy(k_codes[:], picked[:].bitcast(U16).rearrange("p (n o) -> p o n", o=PASSES))
+            dot = ps.tile([P, HALF], F32, name="dot%d" % h, tag="bank%d" % h)
+            for j in range(HALF // TILE):
+                local = slice(j * TILE, (j + 1) * TILE)
+                slots = slice(h * HALF + j * TILE, h * HALF + (j + 1) * TILE)
+                for o in range(PASSES):
+                    nc.tensor.matmul_mx(
+                        out=dot[:, local],
+                        lhsT=q_codes[:, o, :].bitcast(FP8X4),
+                        lhsT_scale=q_planes[:, o, :],
+                        rhs=k_codes[:, o, local].bitcast(FP4X4),
+                        rhs_scale=planes[o][:, slots],
+                        start=(o == 0),
+                        stop=(o == PASSES - 1),
+                    )
+            dots.append(dot)
+
+        roots = []
+        for h in range(2):
+            slots = slice(h * HALF, (h + 1) * HALF)
+            raw = sb.tile([P, HALF], F32, name="raw%d" % h)
+            nc.vector.scalar_tensor_tensor(raw[:], dots[h][:], -2.0, kn_rows[:, slots], ALU.mult, ALU.add)
+            dist = sb.tile([P, HALF], F32, name="dist%d" % h)
+            nc.vector.tensor_scalar(dist[:], raw[:], qn_col[:], 0.0, ALU.add, ALU.max)
+            root = sb.tile([P, HALF], F32, name="root%d" % h)
+            nc.scalar.activation(root[:], dist[:], ACT.Abs_reciprocal_sqrt, bias=1.0)
+            roots.append(root)
+
+        sim0 = sb.tile([P, HALF], F32, name="sim0")
+        sum0 = sb.tile([P, 1], F32, name="sum0")
+        nc.vector.scalar_tensor_tensor(sim0[:], roots[0][:], 1.0, roots[0][:], ALU.mult, ALU.mult, accum_out=sum0[:])
+        sim1 = sb.tile([P, HALF], F32, name="sim1")
+        sum1 = sb.tile([P, 1], F32, name="sum1")
+        nc.scalar.activation(sim1[:], roots[1][:], ACT.Square, accum_out=sum1[:])
+        norm = sb.tile([P, 1], F32, name="norm")
+        nc.scalar.activation(norm[:], sum0[:], ACT.Abs_reciprocal_sqrt, bias=sum1[:])
+
+        for h, sim in enumerate((sim0, sim1)):
+            res = sb.tile([P, HALF], F32, name="res%d" % h)
+            nc.vector.tensor_scalar(res[:], sim[:], norm[:], norm[:], ALU.mult, ALU.mult)
+            queue = nc.sync if h == 0 else nc.scalar
+            queue.dma_start(out[0][:, h * HALF : (h + 1) * HALF], res[:])

@@ -22,99 +22,111 @@ N = 512
 HALF = 256
 TILE = 128
 PASSES = 2
-KN_ROW = 8
+PER_BANK = 4
+BANKS = T // (P * PER_BANK)
 SHIFT = 16
-MOVED_ROWS = 112
+MOVED_ROWS = P - SHIFT
 
 
 def tile_attend_student_topk_kernel(tc, qT, k_words, k_scales, kn, qn, offs, out):
     nc = tc.nc
     with ExitStack() as ctx:
         sb = ctx.enter_context(tc.tile_pool(name="sb", bufs=1))
-        reused = ctx.enter_context(tc.tile_pool(name="reused", bufs=1))
+        after_scales = ctx.enter_context(tc.tile_pool(name="after_scales", bufs=1))
+        after_queries = ctx.enter_context(tc.tile_pool(name="after_queries", bufs=1))
         ps = ctx.enter_context(tc.psum_pool(name="ps", bufs=1))
 
+        kn_runs = after_queries.tile([P, BANKS, PER_BANK], F32, name="kn_runs", offset=1088)
+        nc.sync.dma_start(kn_runs[:], kn[0].rearrange("(p b i) -> p b i", b=BANKS, i=PER_BANK))
         offsets = sb.tile([P, N // 16], U16, name="offsets")
         nc.sync.dma_start(offsets[:], offs)
-        qn_col = sb.tile([P, 1], F32, name="qn_col")
-        nc.sync.dma_start(qn_col[:], qn[0])
 
-        q_raw = sb.tile([P, PASSES, 4, P], F32, name="q_raw")
-        nc.scalar.dma_start(q_raw[:], qT[0].rearrange("(o p j) w -> p o j w", o=PASSES, j=4))
-        scales = sb.tile([P, T], U8, name="scales")
+        q_rows = qT[0].rearrange("(o p j) w -> o p j w", o=PASSES, j=4)
+        q_raw = [sb.tile([P, 4, P], F32, name="q_raw%d" % o) for o in range(PASSES)]
+        words = sb.tile([P, T], I32, name="words")
+        nc.scalar.dma_start(q_raw[0][:], q_rows[0])
+
+        scales = after_scales.tile([P, T], U8, name="scales", offset=0)
         nc.vector.memset(scales[:].bitcast(I32), 0)
         by_row = k_scales.rearrange("o (q r) t -> r q o t", r=4)
         for r in range(4):
             nc.sync.dma_start(scales[r:P:SHIFT, :].bitcast(I32), by_row[r].bitcast(I32))
-        words = sb.tile([P, T], I32, name="words")
         nc.sync.dma_start(words[:], k_words[0].rearrange("p t b -> p (t b)").bitcast(I32))
-
-        kn_all = reused.tile([P, T], F32, name="kn_all", offset=0)
-        nc.vector.memset(kn_all[:], 0.0)
-        nc.scalar.dma_start(kn_all[KN_ROW : KN_ROW + 1, :], kn[0:1, :])
+        nc.sync.dma_start(q_raw[1][:], q_rows[1])
+        qn_col = sb.tile([P, 1], F32, name="qn_col")
+        nc.sync.dma_start(qn_col[:], qn[0])
 
         plane1 = sb.tile([P, N], U8, name="plane1", align_bytes=64)
         nc.vector.memset(plane1[:].bitcast(I32), 0)
 
-        seed = sb.tile([P, 1], F32, name="seed", tag="ident")
-        nc.vector.memset(seed[:], 1.0)
-        warm = sb.tile([P, 1], F32, name="warm")
-        nc.scalar.activation(warm[:], seed[:], ACT.Abs_reciprocal_sqrt, bias=1.0)
-        ident = sb.tile([P, P], F32, name="ident", tag="ident")
+        ident = sb.tile([P, P], F32, name="ident")
         make_identity(nc, ident[:])
 
         plane0 = sb.tile([P, N], U8, name="plane0", align_bytes=64)
         nc.vector.tensor_copy(plane0[:], scales[:].indirect(offsets[:]))
-        nc.sync.dma_start(
-            plane1[0:MOVED_ROWS, :].bitcast(I32),
-            plane0[SHIFT : SHIFT + MOVED_ROWS, :].bitcast(I32),
-        )
+        nc.sync.dma_start(plane1[0:MOVED_ROWS, :].bitcast(I32), plane0[SHIFT:P, :].bitcast(I32))
         planes = (plane0, plane1)
 
-        kn_listed = sb.tile([P, N], F32, name="kn_listed")
-        nc.vector.tensor_copy(kn_listed[:], kn_all[:].indirect(offsets[:]))
+        q_codes = (
+            after_scales.tile([P, P], U32, name="q_codes0", align_bytes=64, offset=1024),
+            sb.tile([P, P], U32, name="q_codes1", align_bytes=64),
+        )
+        q_planes = [sb.tile([P, P], U8, name="q_plane%d" % o, align_bytes=64) for o in range(PASSES)]
 
-        q_codes = reused.tile([P, PASSES, P], U32, name="q_codes", align_bytes=64, offset=0)
-        q_planes = reused.tile([P, PASSES, P], U8, name="q_planes", align_bytes=64, offset=1024)
-        for o in range(PASSES):
-            q_bf = sb.tile([P, P, 4], BF16, name="q_bf%d" % o, align_bytes=64)
-            nc.scalar.copy(
-                q_bf[:].rearrange("p (c i) t -> p c t i", i=4),
-                q_raw[:, o].rearrange("p t (c i) -> p c t i", i=4),
-            )
+        q_staged = (
+            after_scales.tile([P, P, 4], BF16, name="q_bf0", align_bytes=64, offset=0),
+            after_queries.tile([P, P, 4], BF16, name="q_bf1", align_bytes=64, offset=768),
+        )
+
+        def quantise_queries(o):
+            q_bf = q_staged[o]
+            if o == 0:
+                nc.vector.tensor_copy(
+                    q_bf[:].rearrange("p (c i) t -> p c t i", i=4),
+                    q_raw[o][:].rearrange("p t (c i) -> p c t i", i=4),
+                )
+            else:
+                nc.scalar.copy(q_bf[:], q_raw[o][:].rearrange("p t w -> p w t"))
             nc.vector.quantize_mx(
-                out=q_codes[:, o, :].bitcast(FP8X4),
-                scales=q_planes[:, o, :],
+                out=q_codes[o][:].bitcast(FP8X4),
+                scales=q_planes[o][:],
                 in_=q_bf[:].rearrange("p w t -> p (w t)"),
             )
 
-        kn_turned = ps.tile([P, N // TILE, TILE], F32, name="kn_turned", tag="bank0")
-        for j in range(N // TILE):
-            nc.tensor.transpose(kn_turned[:, j, :], kn_listed[:, j * TILE : (j + 1) * TILE], ident[:])
-        kn_cols = sb.tile([P, N // TILE], F32, name="kn_cols")
-        nc.scalar.copy(kn_cols[:], kn_turned[:, :, KN_ROW])
-        kn_spread = ps.tile([P, N // TILE, TILE], F32, name="kn_spread")
-        for j in range(N // TILE):
-            nc.tensor.transpose(kn_spread[:, j, :], kn_cols[:, j : j + 1].to_broadcast([P, P]), ident[:])
-        kn_rows = sb.tile([P, N], F32, name="kn_rows")
-        nc.scalar.copy(kn_rows[:], kn_spread[:].rearrange("p j n -> p (j n)"))
+        quantise_queries(0)
 
+        kn_all = sb.tile([P, T], F32, name="kn_all")
+        for b in range(BANKS):
+            spread = ps.tile([P, PER_BANK, P], F32, name="spread%d" % b, tag="bank%d" % b)
+            for i in range(PER_BANK):
+                nc.tensor.transpose(spread[:, i, :], kn_runs[:, b, i : i + 1].to_broadcast([P, P]), ident[:])
+            nc.scalar.copy(
+                kn_all[:].rearrange("p (n b i) -> p b n i", b=BANKS, i=PER_BANK)[:, b],
+                spread[:].rearrange("p i n -> p n i"),
+            )
+
+        quantise_queries(1)
+
+        lists = [offsets[:, h * HALF // 16 : (h + 1) * HALF // 16] for h in range(2)]
+        gathered = (
+            after_scales.tile([P, HALF], U32, name="picked0", offset=0),
+            after_queries.tile([P, HALF], U32, name="picked1", offset=0),
+        )
         dots = []
         for h in range(2):
-            picked = reused.tile([P, HALF], U32, name="picked%d" % h, offset=2048 + 1024 * h)
-            cols = slice(h * HALF // 16, (h + 1) * HALF // 16)
-            nc.vector.tensor_copy(picked[:], words[:].bitcast(U32).indirect(offsets[:, cols]))
+            picked = gathered[h]
+            nc.vector.tensor_copy(picked[:], words[:].bitcast(U32).indirect(lists[h]))
             k_codes = sb.tile([P, PASSES, HALF], U16, name="k_codes%d" % h, align_bytes=64)
             nc.vector.tensor_copy(k_codes[:], picked[:].bitcast(U16).rearrange("p (n o) -> p o n", o=PASSES))
-            dot = ps.tile([P, HALF], F32, name="dot%d" % h, tag="bank%d" % h)
+            dot = ps.tile([P, HALF], F32, name="dot%d" % h, tag="bank%d" % (2 + h))
             for j in range(HALF // TILE):
                 local = slice(j * TILE, (j + 1) * TILE)
                 slots = slice(h * HALF + j * TILE, h * HALF + (j + 1) * TILE)
                 for o in range(PASSES):
                     nc.tensor.matmul_mx(
                         out=dot[:, local],
-                        lhsT=q_codes[:, o, :].bitcast(FP8X4),
-                        lhsT_scale=q_planes[:, o, :],
+                        lhsT=q_codes[o][:].bitcast(FP8X4),
+                        lhsT_scale=q_planes[o][:],
                         rhs=k_codes[:, o, local].bitcast(FP4X4),
                         rhs_scale=planes[o][:, slots],
                         start=(o == 0),
@@ -122,11 +134,16 @@ def tile_attend_student_topk_kernel(tc, qT, k_words, k_scales, kn, qn, offs, out
                     )
             dots.append(dot)
 
+        kn_halves = (
+            sb.tile([P, HALF], F32, name="kn_listed0"),
+            after_queries.tile([P, HALF], F32, name="kn_listed1", offset=0),
+        )
         roots = []
         for h in range(2):
-            slots = slice(h * HALF, (h + 1) * HALF)
+            kn_listed = kn_halves[h]
+            nc.vector.tensor_copy(kn_listed[:], kn_all[:].indirect(lists[h]))
             raw = sb.tile([P, HALF], F32, name="raw%d" % h)
-            nc.vector.scalar_tensor_tensor(raw[:], dots[h][:], -2.0, kn_rows[:, slots], ALU.mult, ALU.add)
+            nc.vector.scalar_tensor_tensor(raw[:], dots[h][:], -2.0, kn_listed[:], ALU.mult, ALU.add)
             dist = sb.tile([P, HALF], F32, name="dist%d" % h)
             nc.vector.tensor_scalar(dist[:], raw[:], qn_col[:], 0.0, ALU.add, ALU.max)
             root = sb.tile([P, HALF], F32, name="root%d" % h)
@@ -142,8 +159,9 @@ def tile_attend_student_topk_kernel(tc, qT, k_words, k_scales, kn, qn, offs, out
         norm = sb.tile([P, 1], F32, name="norm")
         nc.scalar.activation(norm[:], sum0[:], ACT.Abs_reciprocal_sqrt, bias=sum1[:])
 
-        for h, sim in enumerate((sim0, sim1)):
-            res = sb.tile([P, HALF], F32, name="res%d" % h)
-            nc.vector.tensor_scalar(res[:], sim[:], norm[:], norm[:], ALU.mult, ALU.mult)
-            queue = nc.sync if h == 0 else nc.scalar
-            queue.dma_start(out[0][:, h * HALF : (h + 1) * HALF], res[:])
+        res0 = sb.tile([P, HALF], F32, name="res0")
+        nc.vector.tensor_scalar(res0[:], sim0[:], norm[:], norm[:], ALU.mult, ALU.mult)
+        nc.sync.dma_start(out[0][:, 0:HALF], res0[:])
+        res1 = sb.tile([P, HALF], F32, name="res1")
+        nc.scalar.activation(res1[:], roots[1][:], ACT.Square, scale=norm[:])
+        nc.scalar.dma_start(out[0][:, HALF:N], res1[:])

from contextlib import ExitStack

import concourse.mybir as mybir
from concourse.masks import make_identity

FLOPS = 2 * 128 * 512 * 1024

F32 = mybir.dt.float32
BF16 = mybir.dt.bfloat16
I32 = mybir.dt.int32
U32 = mybir.dt.uint32
U16 = mybir.dt.uint16
U8 = mybir.dt.uint8
FP8X4 = mybir.dt.float8_e4m3fn_x4
FP4X4 = mybir.dt.float4_e2m1fn_x4
ALU = mybir.AluOpType
ACT = mybir.ActivationFunctionType

P = 128
T = 2048
N = 512
HALF = 256
TILE = 128
PASSES = 2
PER_BANK = 4
BANKS = T // (P * PER_BANK)
SHIFT = 16
MOVED_ROWS = P - SHIFT


def tile_attend_student_topk_kernel(tc, qT, k_words, k_scales, kn, qn, offs, out):
    nc = tc.nc
    with ExitStack() as ctx:
        sb = ctx.enter_context(tc.tile_pool(name="sb", bufs=1))
        after_scales = ctx.enter_context(tc.tile_pool(name="after_scales", bufs=1))
        after_queries = ctx.enter_context(tc.tile_pool(name="after_queries", bufs=1))
        ps = ctx.enter_context(tc.psum_pool(name="ps", bufs=1))

        kn_runs = after_queries.tile([P, BANKS, PER_BANK], F32, name="kn_runs", offset=1088)
        nc.sync.dma_start(kn_runs[:], kn[0].rearrange("(p b i) -> p b i", b=BANKS, i=PER_BANK))
        offsets = sb.tile([P, N // 16], U16, name="offsets")
        nc.sync.dma_start(offsets[:], offs)

        q_rows = qT[0].rearrange("(o p j) w -> o p j w", o=PASSES, j=4)
        q_raw = [sb.tile([P, 4, P], F32, name="q_raw%d" % o) for o in range(PASSES)]
        words = sb.tile([P, T], I32, name="words")
        nc.scalar.dma_start(q_raw[0][:], q_rows[0])

        scales = after_scales.tile([P, T], U8, name="scales", offset=0)
        nc.vector.memset(scales[:].bitcast(I32), 0)
        by_row = k_scales.rearrange("o (q r) t -> r q o t", r=4)
        for r in range(4):
            nc.sync.dma_start(scales[r:P:SHIFT, :].bitcast(I32), by_row[r].bitcast(I32))
        nc.sync.dma_start(words[:], k_words[0].rearrange("p t b -> p (t b)").bitcast(I32))
        nc.sync.dma_start(q_raw[1][:], q_rows[1])
        qn_col = sb.tile([P, 1], F32, name="qn_col")
        nc.sync.dma_start(qn_col[:], qn[0])

        plane1 = sb.tile([P, N], U8, name="plane1", align_bytes=64)
        nc.vector.memset(plane1[:].bitcast(I32), 0)

        ident = sb.tile([P, P], F32, name="ident")
        make_identity(nc, ident[:])

        plane0 = sb.tile([P, N], U8, name="plane0", align_bytes=64)
        nc.vector.tensor_copy(plane0[:], scales[:].indirect(offsets[:]))
        nc.sync.dma_start(plane1[0:MOVED_ROWS, :].bitcast(I32), plane0[SHIFT:P, :].bitcast(I32))
        planes = (plane0, plane1)

        q_codes = (
            after_scales.tile([P, P], U32, name="q_codes0", align_bytes=64, offset=1024),
            sb.tile([P, P], U32, name="q_codes1", align_bytes=64),
        )
        q_planes = [sb.tile([P, P], U8, name="q_plane%d" % o, align_bytes=64) for o in range(PASSES)]

        q_staged = (
            after_scales.tile([P, P, 4], BF16, name="q_bf0", align_bytes=64, offset=0),
            after_queries.tile([P, P, 4], BF16, name="q_bf1", align_bytes=64, offset=768),
        )

        def quantise_queries(o):
            q_bf = q_staged[o]
            if o == 0:
                nc.vector.tensor_copy(
                    q_bf[:].rearrange("p (c i) t -> p c t i", i=4),
                    q_raw[o][:].rearrange("p t (c i) -> p c t i", i=4),
                )
            else:
                nc.scalar.copy(q_bf[:], q_raw[o][:].rearrange("p t w -> p w t"))
            nc.vector.quantize_mx(
                out=q_codes[o][:].bitcast(FP8X4),
                scales=q_planes[o][:],
                in_=q_bf[:].rearrange("p w t -> p (w t)"),
            )

        quantise_queries(0)

        kn_all = sb.tile([P, T], F32, name="kn_all")
        for b in range(BANKS):
            spread = ps.tile([P, PER_BANK, P], F32, name="spread%d" % b, tag="bank%d" % b)
            for i in range(PER_BANK):
                nc.tensor.transpose(spread[:, i, :], kn_runs[:, b, i : i + 1].to_broadcast([P, P]), ident[:])
            nc.scalar.copy(
                kn_all[:].rearrange("p (n b i) -> p b n i", b=BANKS, i=PER_BANK)[:, b],
                spread[:].rearrange("p i n -> p n i"),
            )

        quantise_queries(1)

        lists = [offsets[:, h * HALF // 16 : (h + 1) * HALF // 16] for h in range(2)]
        gathered = (
            after_scales.tile([P, HALF], U32, name="picked0", offset=0),
            after_queries.tile([P, HALF], U32, name="picked1", offset=0),
        )
        dots = []
        for h in range(2):
            picked = gathered[h]
            nc.vector.tensor_copy(picked[:], words[:].bitcast(U32).indirect(lists[h]))
            k_codes = sb.tile([P, PASSES, HALF], U16, name="k_codes%d" % h, align_bytes=64)
            nc.vector.tensor_copy(k_codes[:], picked[:].bitcast(U16).rearrange("p (n o) -> p o n", o=PASSES))
            dot = ps.tile([P, HALF], F32, name="dot%d" % h, tag="bank%d" % (2 + h))
            for j in range(HALF // TILE):
                local = slice(j * TILE, (j + 1) * TILE)
                slots = slice(h * HALF + j * TILE, h * HALF + (j + 1) * TILE)
                for o in range(PASSES):
                    nc.tensor.matmul_mx(
                        out=dot[:, local],
                        lhsT=q_codes[o][:].bitcast(FP8X4),
                        lhsT_scale=q_planes[o][:],
                        rhs=k_codes[:, o, local].bitcast(FP4X4),
                        rhs_scale=planes[o][:, slots],
                        start=(o == 0),
                        stop=(o == PASSES - 1),
                    )
            dots.append(dot)

        kn_halves = (
            sb.tile([P, HALF], F32, name="kn_listed0"),
            after_queries.tile([P, HALF], F32, name="kn_listed1", offset=0),
        )
        roots = []
        for h in range(2):
            kn_listed = kn_halves[h]
            nc.vector.tensor_copy(kn_listed[:], kn_all[:].indirect(lists[h]))
            raw = sb.tile([P, HALF], F32, name="raw%d" % h)
            nc.vector.scalar_tensor_tensor(raw[:], dots[h][:], -2.0, kn_listed[:], ALU.mult, ALU.add)
            dist = sb.tile([P, HALF], F32, name="dist%d" % h)
            nc.vector.tensor_scalar(dist[:], raw[:], qn_col[:], 0.0, ALU.add, ALU.max)
            root = sb.tile([P, HALF], F32, name="root%d" % h)
            nc.scalar.activation(root[:], dist[:], ACT.Abs_reciprocal_sqrt, bias=1.0)
            roots.append(root)

        sim0 = sb.tile([P, HALF], F32, name="sim0")
        sum0 = sb.tile([P, 1], F32, name="sum0")
        nc.vector.scalar_tensor_tensor(sim0[:], roots[0][:], 1.0, roots[0][:], ALU.mult, ALU.mult, accum_out=sum0[:])
        sim1 = sb.tile([P, HALF], F32, name="sim1")
        sum1 = sb.tile([P, 1], F32, name="sum1")
        nc.scalar.activation(sim1[:], roots[1][:], ACT.Square, accum_out=sum1[:])
        norm = sb.tile([P, 1], F32, name="norm")
        nc.scalar.activation(norm[:], sum0[:], ACT.Abs_reciprocal_sqrt, bias=sum1[:])

        res0 = sb.tile([P, HALF], F32, name="res0")
        nc.vector.tensor_scalar(res0[:], sim0[:], norm[:], norm[:], ALU.mult, ALU.mult)
        nc.sync.dma_start(out[0][:, 0:HALF], res0[:])
        res1 = sb.tile([P, HALF], F32, name="res1")
        nc.scalar.activation(res1[:], roots[1][:], ACT.Square, scale=norm[:])
        nc.scalar.dma_start(out[0][:, HALF:N], res1[:])
